import numpy as np
import ml_dtypes

BF16 = ml_dtypes.bfloat16


def bf(x):
    return np.asarray(x, np.float32).astype(BF16)


def f32(x):
    return np.asarray(x, np.float32)


def f64(x):
    return np.asarray(x).astype(np.float64)


def striped(idx):
    return np.tile(idx.reshape(-1, 16).T, (8, 1))


S, A, K, M, N, E, Q = 512, 256, 256, 512, 384, 1, 384


def sigmoid(v):
    return 1.0 / (1.0 + np.exp(-v))


def setup_inputs():
    return {"x": bf(np.random.standard_normal((A, S))), "wd": bf(np.random.standard_normal((A, M)) / np.sqrt(A)), "y": bf(np.random.standard_normal((K, N))), "w": bf(np.random.standard_normal((K, M)) / np.sqrt(K)), "b": f32(0.5 * np.random.standard_normal((M, 1))), "offs": striped(np.random.permutation(S)[:N])}


def reference(x, wd, y, w, b, offs):
    idx = offs[:16].T.reshape(-1)
    z = f64(wd).T @ f64(x)
    z[:, idx] += f64(w).T @ f64(y)
    return (z + f64(b)) * sigmoid(z + f64(b))

@@ -1,0 +1,56 @@
+import concourse.mybir as mybir
+
+BF16, F32, U16 = mybir.dt.bfloat16, mybir.dt.float32, mybir.dt.uint16
+SILU = mybir.ActivationFunctionType.Silu
+P = 128
+
+D, S, K, M, N = 256, 512, 256, 512, 384
+FLOPS = 2 * M * D * S + 2 * M * K * N
+
+
+def tile_rows_fillproj_silu_kernel(tc, x, wd, y, w, b, offs, out):
+    nc = tc.nc
+    d_blocks, k_blocks, m_blocks = D // P, K // P, M // P
+
+    with (
+        tc.tile_pool(name="held", bufs=1) as held,
+        tc.psum_pool(name="psum", bufs=1) as psum,
+    ):
+        x_tile = held.tile([P, d_blocks, S], BF16, name="x_tile")
+        wd_tile = held.tile([P, d_blocks, M], BF16, name="wd_tile")
+        y_tile = held.tile([P, k_blocks, N], BF16, name="y_tile")
+        w_tile = held.tile([P, k_blocks, M], BF16, name="w_tile")
+        offsets = held.tile([P, N // 16], U16, name="offsets")
+        bias = held.tile([P, m_blocks], F32, name="bias")
+
+        nc.sync.dma_start(wd_tile[:], wd.rearrange("(i p) m -> p i m", p=P))
+        nc.sync.dma_start(x_tile[:], x.rearrange("(i p) s -> p i s", p=P))
+        nc.sync.dma_start(offsets[:], offs)
+        nc.sync.dma_start(w_tile[:], w.rearrange("(i p) m -> p i m", p=P))
+        nc.sync.dma_start(y_tile[:], y.rearrange("(i p) n -> p i n", p=P))
+        nc.sync.dma_start(bias[:], b.rearrange("(m p) o -> p (m o)", p=P))
+
+        windows = [psum.tile([P, S], F32, name=f"window{m}") for m in range(m_blocks)]
+
+        for d in range(d_blocks):
+            for m in range(m_blocks):
+                nc.tensor.matmul(
+                    windows[m][:],
+                    wd_tile[:, d, m * P : (m + 1) * P],
+                    x_tile[:, d, :],
+                    start=(d == 0),
+                    stop=False,
+                )
+
+        for m in range(m_blocks):
+            for k in range(k_blocks):
+                nc.tensor.matmul(
+                    windows[m][:].indirect(offsets[:]),
+                    w_tile[:, k, m * P : (m + 1) * P],
+                    y_tile[:, k, :],
+                    start=False,
+                    stop=(k == k_blocks - 1),
+                )
+            result = held.tile([P, S], F32, name=f"result{m}")
+            nc.scalar.activation(result[:], windows[m][:], SILU, bias=bias[:, m : m + 1])
+            nc.sync.dma_start(out[m * P : (m + 1) * P, :], result[:])

@@ -6,6 +6,7 @@ P = 128
 
 D, S, K, M, N = 256, 512, 256, 512, 384
 FLOPS = 2 * M * D * S + 2 * M * K * N
+WARM_UPS = 5
 
 
 def tile_rows_fillproj_silu_kernel(tc, x, wd, y, w, b, offs, out):
@@ -29,6 +30,12 @@ def tile_rows_fillproj_silu_kernel(tc, x, wd, y, w, b, offs, out):
         nc.sync.dma_start(w_tile[:], w.rearrange("(i p) m -> p i m", p=P))
         nc.sync.dma_start(y_tile[:], y.rearrange("(i p) n -> p i n", p=P))
         nc.sync.dma_start(bias[:], b.rearrange("(m p) o -> p (m o)", p=P))
+
+        zeros = held.tile([P, S], BF16, name="zeros")
+        nc.vector.memset(zeros[:], 0.0)
+        spare = psum.tile([P, S], F32, name="spare")
+        for i in range(WARM_UPS):
+            nc.tensor.matmul(spare[:], zeros[:, :P], zeros[:], start=True, stop=True)
 
         windows = [psum.tile([P, S], F32, name=f"window{m}") for m in range(m_blocks)]
 

@@ -6,7 +6,7 @@ P = 128
 
 D, S, K, M, N = 256, 512, 256, 512, 384
 FLOPS = 2 * M * D * S + 2 * M * K * N
-WARM_UPS = 5
+WARM_UPS = 8
 
 
 def tile_rows_fillproj_silu_kernel(tc, x, wd, y, w, b, offs, out):
@@ -24,16 +24,18 @@ def tile_rows_fillproj_silu_kernel(tc, x, wd, y, w, b, offs, out):
         offsets = held.tile([P, N // 16], U16, name="offsets")
         bias = held.tile([P, m_blocks], F32, name="bias")
 
-        nc.sync.dma_start(wd_tile[:], wd.rearrange("(i p) m -> p i m", p=P))
-        nc.sync.dma_start(x_tile[:], x.rearrange("(i p) s -> p i s", p=P))
+        for d in range(d_blocks):
+            rows = slice(d * P, (d + 1) * P)
+            nc.sync.dma_start(wd_tile[:, d, :], wd[rows, :])
+            nc.sync.dma_start(x_tile[:, d, :], x[rows, :])
         nc.sync.dma_start(offsets[:], offs)
         nc.sync.dma_start(w_tile[:], w.rearrange("(i p) m -> p i m", p=P))
         nc.sync.dma_start(y_tile[:], y.rearrange("(i p) n -> p i n", p=P))
         nc.sync.dma_start(bias[:], b.rearrange("(m p) o -> p (m o)", p=P))
 
-        zeros = held.tile([P, S], BF16, name="zeros")
+        zeros = held.tile([P, 2 * P], BF16, name="zeros")
         nc.vector.memset(zeros[:], 0.0)
-        spare = psum.tile([P, S], F32, name="spare")
+        spare = psum.tile([P, 2 * P], F32, name="spare")
         for i in range(WARM_UPS):
             nc.tensor.matmul(spare[:], zeros[:, :P], zeros[:], start=True, stop=True)
 

@@ -39,6 +39,11 @@ def tile_rows_fillproj_silu_kernel(tc, x, wd, y, w, b, offs, out):
         for i in range(WARM_UPS):
             nc.tensor.matmul(spare[:], zeros[:, :P], zeros[:], start=True, stop=True)
 
+        early = held.tile([P, 1], F32, name="early")
+        zero = held.tile([P, 1], F32, name="zero")
+        nc.vector.memset(zero[:], 0.0)
+        nc.scalar.activation(early[:], zero[:], SILU, bias=zero[:])
+
         windows = [psum.tile([P, S], F32, name=f"window{m}") for m in range(m_blocks)]
 
         for d in range(d_blocks):

import concourse.mybir as mybir

BF16, F32, U16 = mybir.dt.bfloat16, mybir.dt.float32, mybir.dt.uint16
SILU = mybir.ActivationFunctionType.Silu
P = 128

D, S, K, M, N = 256, 512, 256, 512, 384
FLOPS = 2 * M * D * S + 2 * M * K * N
WARM_UPS = 8


def tile_rows_fillproj_silu_kernel(tc, x, wd, y, w, b, offs, out):
    nc = tc.nc
    d_blocks, k_blocks, m_blocks = D // P, K // P, M // P

    with (
        tc.tile_pool(name="held", bufs=1) as held,
        tc.psum_pool(name="psum", bufs=1) as psum,
    ):
        x_tile = held.tile([P, d_blocks, S], BF16, name="x_tile")
        wd_tile = held.tile([P, d_blocks, M], BF16, name="wd_tile")
        y_tile = held.tile([P, k_blocks, N], BF16, name="y_tile")
        w_tile = held.tile([P, k_blocks, M], BF16, name="w_tile")
        offsets = held.tile([P, N // 16], U16, name="offsets")
        bias = held.tile([P, m_blocks], F32, name="bias")

        for d in range(d_blocks):
            rows = slice(d * P, (d + 1) * P)
            nc.sync.dma_start(wd_tile[:, d, :], wd[rows, :])
            nc.sync.dma_start(x_tile[:, d, :], x[rows, :])
        nc.sync.dma_start(offsets[:], offs)
        nc.sync.dma_start(w_tile[:], w.rearrange("(i p) m -> p i m", p=P))
        nc.sync.dma_start(y_tile[:], y.rearrange("(i p) n -> p i n", p=P))
        nc.sync.dma_start(bias[:], b.rearrange("(m p) o -> p (m o)", p=P))

        zeros = held.tile([P, 2 * P], BF16, name="zeros")
        nc.vector.memset(zeros[:], 0.0)
        spare = psum.tile([P, 2 * P], F32, name="spare")
        for i in range(WARM_UPS):
            nc.tensor.matmul(spare[:], zeros[:, :P], zeros[:], start=True, stop=True)

        early = held.tile([P, 1], F32, name="early")
        zero = held.tile([P, 1], F32, name="zero")
        nc.vector.memset(zero[:], 0.0)
        nc.scalar.activation(early[:], zero[:], SILU, bias=zero[:])

        windows = [psum.tile([P, S], F32, name=f"window{m}") for m in range(m_blocks)]

        for d in range(d_blocks):
            for m in range(m_blocks):
                nc.tensor.matmul(
                    windows[m][:],
                    wd_tile[:, d, m * P : (m + 1) * P],
                    x_tile[:, d, :],
                    start=(d == 0),
                    stop=False,
                )

        for m in range(m_blocks):
            for k in range(k_blocks):
                nc.tensor.matmul(
                    windows[m][:].indirect(offsets[:]),
                    w_tile[:, k, m * P : (m + 1) * P],
                    y_tile[:, k, :],
                    start=False,
                    stop=(k == k_blocks - 1),
                )
            result = held.tile([P, S], F32, name=f"result{m}")
            nc.scalar.activation(result[:], windows[m][:], SILU, bias=bias[:, m : m + 1])
            nc.sync.dma_start(out[m * P : (m + 1) * P, :], result[:])
